import numpy as np
import ml_dtypes


def mxq(x, axis, fmt="e4m3"):
    dtype, down = {"e4m3": (ml_dtypes.float8_e4m3fn, 7), "e5m2": (ml_dtypes.float8_e5m2, 14)}[fmt]
    v = np.moveaxis(np.asarray(x, np.float32).astype(ml_dtypes.bfloat16).astype(np.float64), axis, -1)
    blocks = v.reshape(v.shape[:-1] + (-1, 32))
    amax = np.abs(blocks).max(-1, keepdims=True)
    byte = np.maximum(np.where(amax > 0, np.frexp(amax)[1] - 1 + 127, 0) - down, 1)
    scale = np.exp2(byte - 127.0)
    codes = (blocks / scale).astype(np.float32).astype(dtype).astype(np.float64)
    return np.moveaxis((codes * scale).reshape(v.shape), -1, axis)


WIDE = False


def mx_kscale(k):
    if not WIDE:
        return np.ones(k)
    levels = np.array([10, -10, 5, -5, 0])
    if k % 512:
        return np.exp2(np.random.permutation(np.resize(levels, k // 32))).repeat(32)
    a = np.empty((k // 512, 16))
    for p in range(k // 512):
        a[p, :8] = np.random.permutation(np.resize(levels, 8))
        for g in range(8):
            far = levels[np.abs(levels - a[p, g]) >= 10]
            a[p, g + 8] = far[np.random.randint(len(far))]
    return np.exp2(a.ravel()).repeat(32)


def f64(x):
    return np.asarray(x).astype(np.float64)


def striped(idx):
    return np.tile(idx.reshape(-1, 16).T, (8, 1)).astype(np.uint16)


def unstriped(offs):
    return offs[:16].T.reshape(-1).astype(np.int64)


def pack_weight(w):
    k, n = w.shape
    w = f64(np.asarray(w, np.float32).astype(ml_dtypes.bfloat16)).reshape(k // 32, 32, n)
    amax = np.abs(w).max(1)
    byte = np.clip(np.where(amax > 0, np.frexp(amax)[1] - 1 + 127 - 7, 1), 1, 254)
    scaled = (w * np.exp2(127.0 - byte)[:, None, :]).reshape(k, n).astype(np.float32)
    words = np.ascontiguousarray(scaled.reshape(k // 512, 128, 4, n).transpose(0, 1, 3, 2)).astype(ml_dtypes.float8_e4m3fn).view(np.uint8)
    return words, np.ascontiguousarray(byte.astype(np.uint8).reshape(k // 512, 16, n))


def unpack_weight(words, scales):
    g, p, n, _ = words.shape
    vals = np.ascontiguousarray(words).view(ml_dtypes.float8_e4m3fn).astype(np.float64) * np.repeat(np.exp2(scales.astype(np.float64) - 127.0), 8, axis=1)[..., None]
    return vals.transpose(0, 1, 3, 2).reshape(g * 512, n)


def sigmoid(v):
    return 1.0 / (1.0 + np.exp(-np.maximum(v, -700.0)))


K, T, S, H, Z, W = 512, 1024, 512, 512, 512, 2048
P = 2 ** 7


def setup_inputs():
    n = np.random.standard_normal
    s = mx_kscale(K)[:, None]
    u = mx_kscale(H)
    packed_xT = pack_weight(n((K, T)) * s)
    packed_eT = pack_weight(n((K, W)) * s)
    return {
        "x_words": packed_xT[0],
        "x_scales": packed_xT[1],
        "w1": (n((K, H)) / np.sqrt(K) / s).astype(np.float32),
        "w2": (n((K, H)) / np.sqrt(K) / s).astype(np.float32),
        "e_words": packed_eT[0],
        "e_scales": packed_eT[1],
        "w3": (n((K, H)) / np.sqrt(K) / s).astype(np.float32),
        "unit": (np.random.uniform(0.6, 1.4, (H, 1)) * u[:, None]).astype(np.float32),
        "unit2": (np.random.uniform(0.6, 1.4, (H, 1)) / np.sqrt(H) / u[:, None]).astype(np.float32),
        "dt": (np.tile(np.random.uniform(0.1, 1.5, W), (P, 1))).astype(np.float32),
        "offs": striped(np.random.permutation(T)[:S]),
        "tgt": striped(np.random.permutation(W)[:Z]),
        "ls": striped(np.random.permutation(S)),
        "neg_": striped(np.random.permutation(Z)),
    }


def reference(x_words, x_scales, w1, w2, e_words, e_scales, w3, unit, unit2, dt, offs, tgt, ls, neg_):
    xq = unpack_weight(x_words, x_scales)[:, unstriped(offs)]
    y = mxq(f64(w1), 0, "e4m3").T @ xq
    yg = mxq(f64(w2), 0, "e4m3").T @ xq
    yl = y[:, unstriped(ls)]
    upd = y * sigmoid(yg) + 0.5 * yl
    hid = f64(unit) * upd
    e_tgt = unpack_weight(e_words, e_scales)[:, unstriped(tgt)]
    ye = mxq(f64(w3), 0, "e4m3").T @ e_tgt
    tst = np.tanh(ye) + 0.3 * ye
    hid2 = f64(unit2) * tst
    sc = mxq(hid, 0, "e4m3").T @ mxq(hid2, 0, "e4m3")
    dec = sc * (np.exp(-1.0 * (f64(dt)[:1][:, unstriped(tgt)])))
    marg = dec[:, unstriped(neg_)] - dec
    return np.log(np.exp(1.5 * np.tanh(marg)) + 0.5)

@@ -1,0 +1,235 @@
+from contextlib import ExitStack
+
+import concourse.mybir as mybir
+
+F32 = mybir.dt.float32
+BF16 = mybir.dt.bfloat16
+I32 = mybir.dt.int32
+U32 = mybir.dt.uint32
+U16 = mybir.dt.uint16
+U8 = mybir.dt.uint8
+FP8X4 = mybir.dt.float8_e4m3fn_x4
+ACT = mybir.ActivationFunctionType
+ALU = mybir.AluOpType
+
+P = 128
+PACK = 4
+K, T, S, H, Z, W = 512, 1024, 512, 512, 512, 2048
+HALF = 256
+FLOPS = 2 * K * H * S * 2 + 2 * K * H * Z + 2 * H * S * Z
+
+W3_ON_SCALAR = 32
+W1_ON_SCALAR = 48
+W2_ON_SCALAR = 44
+
+
+def tile_picked_ylnkpr_rank_p_kernel(
+    tc, x_words, x_scales, w1, w2, e_words, e_scales, w3, unit, unit2, dt, offs, tgt, ls, neg_, out
+):
+    nc = tc.nc
+    with ExitStack() as ctx:
+        keep = ctx.enter_context(tc.tile_pool(name="keep", bufs=1))
+        psum = ctx.enter_context(tc.psum_pool(name="psum", bufs=1))
+
+        def load_list(name, dram):
+            held = keep.tile([P, dram.shape[1]], U16, name=name)
+            nc.sync.dma_start(held[:], dram)
+            return held
+
+        def load_words(name, dram, width):
+            table = keep.tile([P, width], I32, name=name)
+            nc.sync.dma_start(table[:], dram[0].rearrange("p n t -> p (n t)").bitcast(I32))
+            return table
+
+        def load_scales(queue, table, dram):
+            for q in range(4):
+                queue.dma_start(
+                    table[32 * q : 32 * q + 4, :].bitcast(I32), dram[0, 4 * q : 4 * q + 4, :].bitcast(I32)
+                )
+
+        def load_weight(name, dram):
+            raw = keep.tile([P, PACK, H], F32, name=name)
+            nc.sync.dma_start(raw[:], dram.rearrange("(p j) c -> p j c", j=PACK))
+            return raw
+
+        def load_factors(name, dram):
+            held = keep.tile([P, PACK], F32, name=name)
+            nc.sync.dma_start(held[:], dram.rearrange("(p t) o -> p (t o)", t=PACK))
+            return held
+
+        def gather(name, table, dtype, offsets):
+            picked = keep.tile([P, S], dtype, name=name, align_bytes=64)
+            nc.vector.tensor_copy(picked[:], table.indirect(offsets[:]))
+            return picked
+
+        def cast_weight(name, raw, on_scalar):
+            grouped = keep.tile([P, PACK, P, PACK], BF16, name=name, align_bytes=64)
+            dst = grouped[:].rearrange("p t m j -> p m j t")
+            src = raw[:].rearrange("p j (m t) -> p m j t", t=PACK)
+            if on_scalar > 0:
+                nc.scalar.copy(dst[:, :on_scalar], src[:, :on_scalar])
+            nc.vector.tensor_copy(dst[:, on_scalar:], src[:, on_scalar:])
+            return grouped
+
+        def quantize(name, values, width):
+            codes = keep.tile([P, width], U32, name=name + "_codes", align_bytes=64)
+            scales = keep.tile([P, width], U8, name=name + "_scales", align_bytes=64)
+            nc.vector.quantize_mx(out=codes[:].bitcast(FP8X4), scales=scales[:], in_=values)
+            return codes, scales
+
+        def product(acc, lhs, lhs_cols, rhs, rhs_cols):
+            nc.tensor.matmul_mx(
+                out=acc,
+                lhsT=lhs[0][:, lhs_cols].bitcast(FP8X4),
+                lhsT_scale=lhs[1][:, lhs_cols],
+                rhs=rhs[0][:, rhs_cols].bitcast(FP8X4),
+                rhs_scale=rhs[1][:, rhs_cols],
+                start=True,
+                stop=True,
+            )
+
+        def block(n):
+            return slice(n * P, (n + 1) * P)
+
+        def list_half(held, h):
+            return held[:, h * (HALF // 16) : (h + 1) * (HALF // 16)]
+
+        def half(h):
+            return slice(h * HALF, (h + 1) * HALF)
+
+        xs_table = keep.tile([P, T], U8, name="xs_table")
+        es_table = keep.tile([P, W], U8, name="es_table")
+        nc.gpsimd.memset(xs_table[:].bitcast(I32), 0)
+        nc.gpsimd.memset(es_table[:].bitcast(I32), 0)
+
+        offs_sb = load_list("offs_sb", offs)
+        load_scales(nc.sync, xs_table, x_scales)
+        xw_table = load_words("xw_table", x_words, T)
+        w1_raw = load_weight("w1_raw", w1)
+        tgt_sb = load_list("tgt_sb", tgt)
+        w2_raw = load_weight("w2_raw", w2)
+        load_scales(nc.sync, es_table, e_scales)
+        ls_sb = load_list("ls_sb", ls)
+        unit_sb = load_factors("unit_sb", unit)
+        w3_raw = load_weight("w3_raw", w3)
+        ew_table = load_words("ew_table", e_words, W)
+        unit2_sb = load_factors("unit2_sb", unit2)
+        neg_sb = load_list("neg_sb", neg_)
+        dt_sb = keep.tile([P, W], F32, name="dt_sb")
+        nc.sync.dma_start(dt_sb[:], dt)
+        half_unit = keep.tile([P, PACK], F32, name="half_unit")
+        nc.gpsimd.tensor_scalar(half_unit[:], unit_sb[:], 0.5, 0.0, ALU.mult, ALU.add)
+
+        xs = gather("xs", xs_table[:], U8, offs_sb)
+        xw = gather("xw", xw_table[:].bitcast(U32), U32, offs_sb)
+        w1_b = cast_weight("w1_b", w1_raw, W1_ON_SCALAR)
+        xq = (xw, xs)
+        w1q = quantize("w1", w1_b[:].rearrange("p t m j -> p (t m j)"), H)
+        y_banks = []
+        for t in range(PACK):
+            bank = psum.tile([P, S], F32, name="y%d" % t, tag="b%d" % t)
+            product(bank[:], w1q, block(t), xq, slice(0, S))
+            y_banks.append(bank)
+        w2_b = cast_weight("w2_b", w2_raw, W2_ON_SCALAR)
+        y_half = [keep.tile([P, S], F32, name="y_half%d" % t) for t in range(PACK)]
+        w2q = quantize("w2", w2_b[:].rearrange("p t m j -> p (t m j)"), H)
+        yg_banks = []
+        for t in range(PACK):
+            bank = psum.tile([P, S], F32, name="yg%d" % t, tag="a%d" % t)
+            product(bank[:], w2q, block(t), xq, slice(0, S))
+            yg_banks.append(bank)
+        for t in range(PACK):
+            nc.scalar.activation(y_half[t][:], y_banks[t][:], ACT.Copy, scale=half_unit[:, t : t + 1])
+        w3_b = cast_weight("w3_b", w3_raw, W3_ON_SCALAR)
+        w3q = quantize("w3", w3_b[:].rearrange("p t m j -> p (t m j)"), H)
+        es = gather("es", es_table[:], U8, tgt_sb)
+        ew = gather("ew", ew_table[:].bitcast(U32), U32, tgt_sb)
+        eq = (ew, es)
+
+        gated = keep.tile([P, PACK, S], F32, name="gated")
+        for t in range(PACK):
+            plane = keep.tile([P, S], F32, name="tanh_yg%d" % t)
+            nc.scalar.activation(plane[:], yg_banks[t][:], ACT.Tanh, scale=0.5)
+            nc.vector.scalar_tensor_tensor(gated[:, t, :], plane[:], 1.0, y_half[t][:], ALU.add, ALU.mult)
+
+        hid2_b = keep.tile([P, Z, PACK], BF16, name="hid2_b", align_bytes=64)
+        tst = []
+        for c in range(4):
+            bank = psum.tile([P, PACK, P], F32, name="ye%d" % c, tag="b%d" % c)
+            for t in range(PACK):
+                product(bank[:, t, :], w3q, block(t), eq, block(c))
+            ye = bank[:].rearrange("p t n -> p n t")
+            tanh_ye = keep.tile([P, P, PACK], F32, name="tanh_ye%d" % c)
+            nc.scalar.activation(tanh_ye[:], ye, ACT.Tanh)
+            total = keep.tile([P, P, PACK], F32, name="tst%d" % c)
+            nc.vector.scalar_tensor_tensor(total[:], ye, 0.3, tanh_ye[:], ALU.mult, ALU.add)
+            tst.append(total)
+        for c in range(4):
+            nc.vector.tensor_tensor(
+                hid2_b[:, block(c), :], tst[c][:], unit2_sb[:].unsqueeze(1).to_broadcast([P, P, PACK]), ALU.mult
+            )
+
+        def hid_half(h):
+            picked = keep.tile([P, PACK, HALF], F32, name="picked%d" % h)
+            for t in range(PACK):
+                nc.scalar.activation(picked[:, t, :], y_half[t][:].indirect(list_half(ls_sb, h)), ACT.Copy)
+            hid_b = keep.tile([P, HALF, PACK], BF16, name="hid_b%d" % h, align_bytes=64)
+            nc.vector.tensor_tensor(
+                hid_b[:].rearrange("p (c i) t -> p c t i", i=4),
+                gated[:, :, half(h)].rearrange("p t (c i) -> p c t i", i=4),
+                picked[:].rearrange("p t (c i) -> p c t i", i=4),
+                ALU.add,
+            )
+            return hid_b
+
+        hid_b0 = hid_half(0)
+        hid2q = quantize("hid2", hid2_b[:].rearrange("p n t -> p (n t)"), Z)
+        fade = keep.tile([P, Z], F32, name="fade")
+        nc.scalar.activation(fade[:], dt_sb[:].indirect(tgt_sb[:]), ACT.Exp, scale=-1.0)
+
+        staged = keep.tile([P, 4, Z], F32, name="staged")
+        grown = keep.tile([P, 4, Z], F32, name="grown")
+
+        def scores(r, hidq):
+            bank = psum.tile([P, Z], F32, name="sc%d" % r, tag="a%d" % r)
+            product(bank[:], hidq, block(r % 2), hid2q, slice(0, Z))
+            dec = keep.tile([P, Z], F32, name="dec%d" % r)
+            nc.vector.tensor_tensor(dec[:], bank[:], fade[:], ALU.mult)
+            return dec
+
+        def tanh_exp(r, marg, first, count):
+            cols = slice(first, first + count)
+            bounded = staged[:, :, r * P + first // 4 : r * P + (first + count) // 4]
+            nc.scalar.activation(bounded, marg[:, cols].rearrange("p (a n) -> p a n", a=4), ACT.Tanh)
+            nc.scalar.activation(grown[:, r, cols].rearrange("p (a n) -> p a n", a=4), bounded, ACT.Exp, scale=1.5)
+
+        other = [keep.tile([P, Z], F32, name="other%d" % r) for r in range(4)]
+        marg = [keep.tile([P, Z], F32, name="marg%d" % r) for r in range(4)]
+
+        def fused_margin(r, dec, h):
+            nc.vector.tensor_tensor(
+                marg[r][:, half(h)], dec[:].indirect(list_half(neg_sb, h)), other[r][:, half(h)], ALU.subtract
+            )
+            tanh_exp(r, marg[r], h * HALF, HALF)
+
+        hidq0 = quantize("hid0", hid_b0[:].rearrange("p n t -> p (n t)"), HALF)
+        hid_b1 = hid_half(1)
+        decs = [scores(r, hidq0) for r in range(2)]
+        hidq1 = quantize("hid1", hid_b1[:].rearrange("p n t -> p (n t)"), HALF)
+        nc.scalar.copy(other[0][:], decs[0][:])
+        for h in range(2):
+            fused_margin(0, decs[0], h)
+        for h in range(2):
+            nc.scalar.activation(other[1][:, half(h)], decs[1][:].indirect(list_half(neg_sb, h)), ACT.Copy)
+        nc.vector.tensor_tensor(marg[1][:], other[1][:], decs[1][:], ALU.subtract)
+        tanh_exp(1, marg[1], 0, Z)
+        decs = decs + [scores(r, hidq1) for r in range(2, 4)]
+        for r in range(2, 4):
+            nc.vector.tensor_copy(other[r][:], decs[r][:])
+        for h in range(2):
+            for r in range(2, 4):
+                fused_margin(r, decs[r], h)
+
+        for r in range(4):
+            nc.scalar.activation(staged[:, r, :], grown[:, r, :], ACT.Ln, bias=0.5)
+            nc.sync.dma_start(out[block(r), :], staged[:, r, :])

@@ -18,9 +18,9 @@ K, T, S, H, Z, W = 512, 1024, 512, 512, 512, 2048
 HALF = 256
 FLOPS = 2 * K * H * S * 2 + 2 * K * H * Z + 2 * H * S * Z
 
-W3_ON_SCALAR = 32
+W3_ON_SCALAR = 44
 W1_ON_SCALAR = 48
-W2_ON_SCALAR = 44
+W2_ON_SCALAR = 0
 
 
 def tile_picked_ylnkpr_rank_p_kernel(
@@ -37,7 +37,7 @@ def tile_picked_ylnkpr_rank_p_kernel(
             return held
 
         def load_words(name, dram, width):
-            table = keep.tile([P, width], I32, name=name)
+            table = keep.tile([P, width], I32, name=name, tag=name)
             nc.sync.dma_start(table[:], dram[0].rearrange("p n t -> p (n t)").bitcast(I32))
             return table
 
@@ -48,7 +48,7 @@ def tile_picked_ylnkpr_rank_p_kernel(
                 )
 
         def load_weight(name, dram):
-            raw = keep.tile([P, PACK, H], F32, name=name)
+            raw = keep.tile([P, PACK, H], F32, name=name, tag=name)
             nc.sync.dma_start(raw[:], dram.rearrange("(p j) c -> p j c", j=PACK))
             return raw
 
@@ -57,13 +57,13 @@ def tile_picked_ylnkpr_rank_p_kernel(
             nc.sync.dma_start(held[:], dram.rearrange("(p t) o -> p (t o)", t=PACK))
             return held
 
-        def gather(name, table, dtype, offsets):
-            picked = keep.tile([P, S], dtype, name=name, align_bytes=64)
+        def gather(name, table, dtype, offsets, tag):
+            picked = keep.tile([P, S], dtype, name=name, tag=tag, align_bytes=64)
             nc.vector.tensor_copy(picked[:], table.indirect(offsets[:]))
             return picked
 
         def cast_weight(name, raw, on_scalar):
-            grouped = keep.tile([P, PACK, P, PACK], BF16, name=name, align_bytes=64)
+            grouped = keep.tile([P, PACK, P, PACK], BF16, name=name, tag=name, align_bytes=64)
             dst = grouped[:].rearrange("p t m j -> p m j t")
             src = raw[:].rearrange("p j (m t) -> p m j t", t=PACK)
             if on_scalar > 0:
@@ -107,10 +107,10 @@ def tile_picked_ylnkpr_rank_p_kernel(
         xw_table = load_words("xw_table", x_words, T)
         w1_raw = load_weight("w1_raw", w1)
         tgt_sb = load_list("tgt_sb", tgt)
-        w2_raw = load_weight("w2_raw", w2)
         load_scales(nc.sync, es_table, e_scales)
-        ls_sb = load_list("ls_sb", ls)
         unit_sb = load_factors("unit_sb", unit)
+        w2_raw = load_weight("w2_raw", w2)
+        ls_sb = load_list("ls_sb", ls)
         w3_raw = load_weight("w3_raw", w3)
         ew_table = load_words("ew_table", e_words, W)
         unit2_sb = load_factors("unit2_sb", unit2)
@@ -120,8 +120,8 @@ def tile_picked_ylnkpr_rank_p_kernel(
         half_unit = keep.tile([P, PACK], F32, name="half_unit")
         nc.gpsimd.tensor_scalar(half_unit[:], unit_sb[:], 0.5, 0.0, ALU.mult, ALU.add)
 
-        xs = gather("xs", xs_table[:], U8, offs_sb)
-        xw = gather("xw", xw_table[:].bitcast(U32), U32, offs_sb)
+        xs = gather("xs", xs_table[:], U8, offs_sb, "xs")
+        xw = gather("xw", xw_table[:].bitcast(U32), U32, offs_sb, "xw")
         w1_b = cast_weight("w1_b", w1_raw, W1_ON_SCALAR)
         xq = (xw, xs)
         w1q = quantize("w1", w1_b[:].rearrange("p t m j -> p (t m j)"), H)
@@ -131,35 +131,37 @@ def tile_picked_ylnkpr_rank_p_kernel(
             product(bank[:], w1q, block(t), xq, slice(0, S))
             y_banks.append(bank)
         w2_b = cast_weight("w2_b", w2_raw, W2_ON_SCALAR)
-        y_half = [keep.tile([P, S], F32, name="y_half%d" % t) for t in range(PACK)]
+        y_half = keep.tile([P, PACK, S], F32, name="y_half")
         w2q = quantize("w2", w2_b[:].rearrange("p t m j -> p (t m j)"), H)
         yg_banks = []
         for t in range(PACK):
             bank = psum.tile([P, S], F32, name="yg%d" % t, tag="a%d" % t)
             product(bank[:], w2q, block(t), xq, slice(0, S))
             yg_banks.append(bank)
-        for t in range(PACK):
-            nc.scalar.activation(y_half[t][:], y_banks[t][:], ACT.Copy, scale=half_unit[:, t : t + 1])
         w3_b = cast_weight("w3_b", w3_raw, W3_ON_SCALAR)
         w3q = quantize("w3", w3_b[:].rearrange("p t m j -> p (t m j)"), H)
-        es = gather("es", es_table[:], U8, tgt_sb)
-        ew = gather("ew", ew_table[:].bitcast(U32), U32, tgt_sb)
+        for t in range(PACK):
+            nc.scalar.activation(y_half[:, t, :], y_banks[t][:], ACT.Copy, scale=half_unit[:, t : t + 1])
+        es = gather("es", es_table[:], U8, tgt_sb, "w1_b")
+        ew = gather("ew", ew_table[:].bitcast(U32), U32, tgt_sb, "ew")
         eq = (ew, es)
 
-        gated = keep.tile([P, PACK, S], F32, name="gated")
+        tanh_yg = keep.tile([P, PACK, S], F32, name="tanh_yg", tag="w3_raw")
+        gated0 = keep.tile([P, PACK, HALF], F32, name="gated0", tag="ew_table")
         for t in range(PACK):
-            plane = keep.tile([P, S], F32, name="tanh_yg%d" % t)
-            nc.scalar.activation(plane[:], yg_banks[t][:], ACT.Tanh, scale=0.5)
-            nc.vector.scalar_tensor_tensor(gated[:, t, :], plane[:], 1.0, y_half[t][:], ALU.add, ALU.mult)
+            nc.scalar.activation(tanh_yg[:, t, :], yg_banks[t][:], ACT.Tanh, scale=0.5)
+            nc.vector.scalar_tensor_tensor(
+                gated0[:, t, :], tanh_yg[:, t, half(0)], 1.0, y_half[:, t, half(0)], ALU.add, ALU.mult
+            )
 
-        hid2_b = keep.tile([P, Z, PACK], BF16, name="hid2_b", align_bytes=64)
+        hid2_b = keep.tile([P, Z, PACK], BF16, name="hid2_b", tag="hid2_b", align_bytes=64)
         tst = []
         for c in range(4):
             bank = psum.tile([P, PACK, P], F32, name="ye%d" % c, tag="b%d" % c)
             for t in range(PACK):
                 product(bank[:, t, :], w3q, block(t), eq, block(c))
             ye = bank[:].rearrange("p t n -> p n t")
-            tanh_ye = keep.tile([P, P, PACK], F32, name="tanh_ye%d" % c)
+            tanh_ye = keep.tile([P, P, PACK], F32, name="tanh_ye%d" % c, tag=("picked0", "picked1", "fade", "ye3")[c])
             nc.scalar.activation(tanh_ye[:], ye, ACT.Tanh)
             total = keep.tile([P, P, PACK], F32, name="tst%d" % c)
             nc.vector.scalar_tensor_tensor(total[:], ye, 0.3, tanh_ye[:], ALU.mult, ALU.add)
@@ -169,22 +171,25 @@ def tile_picked_ylnkpr_rank_p_kernel(
                 hid2_b[:, block(c), :], tst[c][:], unit2_sb[:].unsqueeze(1).to_broadcast([P, P, PACK]), ALU.mult
             )
 
-        def hid_half(h):
-            picked = keep.tile([P, PACK, HALF], F32, name="picked%d" % h)
+        def pick_half(h):
+            picked = keep.tile([P, PACK, HALF], F32, name="picked%d" % h, tag="picked%d" % h)
             for t in range(PACK):
-                nc.scalar.activation(picked[:, t, :], y_half[t][:].indirect(list_half(ls_sb, h)), ACT.Copy)
+                nc.scalar.activation(picked[:, t, :], y_half[:, t, :].indirect(list_half(ls_sb, h)), ACT.Copy)
+            return picked
+
+        def hid_half(h, gated, picked):
             hid_b = keep.tile([P, HALF, PACK], BF16, name="hid_b%d" % h, align_bytes=64)
             nc.vector.tensor_tensor(
                 hid_b[:].rearrange("p (c i) t -> p c t i", i=4),
-                gated[:, :, half(h)].rearrange("p t (c i) -> p c t i", i=4),
+                gated[:].rearrange("p t (c i) -> p c t i", i=4),
                 picked[:].rearrange("p t (c i) -> p c t i", i=4),
                 ALU.add,
             )
             return hid_b
 
-        hid_b0 = hid_half(0)
+        hid_b0 = hid_half(0, gated0, pick_half(0))
         hid2q = quantize("hid2", hid2_b[:].rearrange("p n t -> p (n t)"), Z)
-        fade = keep.tile([P, Z], F32, name="fade")
+        fade = keep.tile([P, Z], F32, name="fade", tag="fade")
         nc.scalar.activation(fade[:], dt_sb[:].indirect(tgt_sb[:]), ACT.Exp, scale=-1.0)
 
         staged = keep.tile([P, 4, Z], F32, name="staged")
@@ -197,39 +202,50 @@ def tile_picked_ylnkpr_rank_p_kernel(
             nc.vector.tensor_tensor(dec[:], bank[:], fade[:], ALU.mult)
             return dec
 
-        def tanh_exp(r, marg, first, count):
-            cols = slice(first, first + count)
-            bounded = staged[:, :, r * P + first // 4 : r * P + (first + count) // 4]
-            nc.scalar.activation(bounded, marg[:, cols].rearrange("p (a n) -> p a n", a=4), ACT.Tanh)
-            nc.scalar.activation(grown[:, r, cols].rearrange("p (a n) -> p a n", a=4), bounded, ACT.Exp, scale=1.5)
+        def spread(r, first, count):
+            return staged[:, :, r * P + first // 4 : r * P + (first + count) // 4]
+
+        def bound(r, first, count):
+            source = marg[r][:, first : first + count].rearrange("p (a n) -> p a n", a=4)
+            nc.scalar.activation(spread(r, first, count), source, ACT.Tanh)
+
+        def grow(r, first, count):
+            target = grown[:, r, first : first + count].rearrange("p (a n) -> p a n", a=4)
+            nc.scalar.activation(target, spread(r, first, count), ACT.Exp, scale=1.5)
 
         other = [keep.tile([P, Z], F32, name="other%d" % r) for r in range(4)]
         marg = [keep.tile([P, Z], F32, name="marg%d" % r) for r in range(4)]
 
-        def fused_margin(r, dec, h):
-            nc.vector.tensor_tensor(
-                marg[r][:, half(h)], dec[:].indirect(list_half(neg_sb, h)), other[r][:, half(h)], ALU.subtract
-            )
-            tanh_exp(r, marg[r], h * HALF, HALF)
-
         hidq0 = quantize("hid0", hid_b0[:].rearrange("p n t -> p (n t)"), HALF)
-        hid_b1 = hid_half(1)
+        picked1 = pick_half(1)
+        gated1 = keep.tile([P, PACK, HALF], F32, name="gated1", tag="hid2_b", align_bytes=64)
+        nc.vector.scalar_tensor_tensor(gated1[:], tanh_yg[:, :, half(1)], 1.0, y_half[:, :, half(1)], ALU.add, ALU.mult)
         decs = [scores(r, hidq0) for r in range(2)]
+        hid_b1 = hid_half(1, gated1, picked1)
         hidq1 = quantize("hid1", hid_b1[:].rearrange("p n t -> p (n t)"), HALF)
-        nc.scalar.copy(other[0][:], decs[0][:])
-        for h in range(2):
-            fused_margin(0, decs[0], h)
-        for h in range(2):
-            nc.scalar.activation(other[1][:, half(h)], decs[1][:].indirect(list_half(neg_sb, h)), ACT.Copy)
-        nc.vector.tensor_tensor(marg[1][:], other[1][:], decs[1][:], ALU.subtract)
-        tanh_exp(1, marg[1], 0, Z)
+        for r in range(2):
+            for h in range(2):
+                nc.scalar.activation(other[r][:, half(h)], decs[r][:].indirect(list_half(neg_sb, h)), ACT.Copy)
+            nc.vector.tensor_tensor(marg[r][:], other[r][:], decs[r][:], ALU.subtract)
+        for r in range(2):
+            bound(r, 0, Z)
+        for r in range(2):
+            grow(r, 0, Z)
         decs = decs + [scores(r, hidq1) for r in range(2, 4)]
         for r in range(2, 4):
             nc.vector.tensor_copy(other[r][:], decs[r][:])
         for h in range(2):
             for r in range(2, 4):
-                fused_margin(r, decs[r], h)
+                nc.vector.tensor_tensor(
+                    marg[r][:, half(h)], decs[r][:].indirect(list_half(neg_sb, h)), other[r][:, half(h)], ALU.subtract
+                )
+                bound(r, h * HALF, HALF)
+            for r in range(2, 4):
+                grow(r, h * HALF, HALF)
 
-        for r in range(4):
+        for r in range(3):
             nc.scalar.activation(staged[:, r, :], grown[:, r, :], ACT.Ln, bias=0.5)
             nc.sync.dma_start(out[block(r), :], staged[:, r, :])
+        for h in range(2):
+            nc.scalar.activation(staged[:, 3, half(h)], grown[:, 3, half(h)], ACT.Ln, bias=0.5)
+            nc.sync.dma_start(out[block(3), half(h)], staged[:, 3, half(h)])

@@ -41,11 +41,9 @@ def tile_picked_ylnkpr_rank_p_kernel(
             nc.sync.dma_start(table[:], dram[0].rearrange("p n t -> p (n t)").bitcast(I32))
             return table
 
-        def load_scales(queue, table, dram):
-            for q in range(4):
-                queue.dma_start(
-                    table[32 * q : 32 * q + 4, :].bitcast(I32), dram[0, 4 * q : 4 * q + 4, :].bitcast(I32)
-                )
+        def load_scales(queue, table, dram, first):
+            for r in range(4):
+                queue.dma_start(table[first + r : P : 32, :].bitcast(I32), dram[0, r:16:4, :].bitcast(I32))
 
         def load_weight(name, dram):
             raw = keep.tile([P, PACK, H], F32, name=name, tag=name)
@@ -102,12 +100,12 @@ def tile_picked_ylnkpr_rank_p_kernel(
         nc.gpsimd.memset(xs_table[:].bitcast(I32), 0)
         nc.gpsimd.memset(es_table[:].bitcast(I32), 0)
 
-        offs_sb = load_list("offs_sb", offs)
-        load_scales(nc.sync, xs_table, x_scales)
         xw_table = load_words("xw_table", x_words, T)
+        offs_sb = load_list("offs_sb", offs)
+        load_scales(nc.sync, xs_table, x_scales, 4)
         w1_raw = load_weight("w1_raw", w1)
         tgt_sb = load_list("tgt_sb", tgt)
-        load_scales(nc.sync, es_table, e_scales)
+        load_scales(nc.sync, es_table, e_scales, 0)
         unit_sb = load_factors("unit_sb", unit)
         w2_raw = load_weight("w2_raw", w2)
         ls_sb = load_list("ls_sb", ls)
@@ -120,10 +118,10 @@ def tile_picked_ylnkpr_rank_p_kernel(
         half_unit = keep.tile([P, PACK], F32, name="half_unit")
         nc.gpsimd.tensor_scalar(half_unit[:], unit_sb[:], 0.5, 0.0, ALU.mult, ALU.add)
 
-        xs = gather("xs", xs_table[:], U8, offs_sb, "xs")
         xw = gather("xw", xw_table[:].bitcast(U32), U32, offs_sb, "xw")
+        xs = gather("xs", xs_table[:], U8, offs_sb, "xs")
         w1_b = cast_weight("w1_b", w1_raw, W1_ON_SCALAR)
-        xq = (xw, xs)
+        xq = (xw, xs[4:P])
         w1q = quantize("w1", w1_b[:].rearrange("p t m j -> p (t m j)"), H)
         y_banks = []
         for t in range(PACK):
@@ -180,9 +178,9 @@ def tile_picked_ylnkpr_rank_p_kernel(
         def hid_half(h, gated, picked):
             hid_b = keep.tile([P, HALF, PACK], BF16, name="hid_b%d" % h, align_bytes=64)
             nc.vector.tensor_tensor(
-                hid_b[:].rearrange("p (c i) t -> p c t i", i=4),
-                gated[:].rearrange("p t (c i) -> p c t i", i=4),
-                picked[:].rearrange("p t (c i) -> p c t i", i=4),
+                hid_b[:].rearrange("p (c i) t -> p c t i", i=2),
+                gated[:].rearrange("p t (c i) -> p c t i", i=2),
+                picked[:].rearrange("p t (c i) -> p c t i", i=2),
                 ALU.add,
             )
             return hid_b

from contextlib import ExitStack

import concourse.mybir as mybir

F32 = mybir.dt.float32
BF16 = mybir.dt.bfloat16
I32 = mybir.dt.int32
U32 = mybir.dt.uint32
U16 = mybir.dt.uint16
U8 = mybir.dt.uint8
FP8X4 = mybir.dt.float8_e4m3fn_x4
ACT = mybir.ActivationFunctionType
ALU = mybir.AluOpType

P = 128
PACK = 4
K, T, S, H, Z, W = 512, 1024, 512, 512, 512, 2048
HALF = 256
FLOPS = 2 * K * H * S * 2 + 2 * K * H * Z + 2 * H * S * Z

W3_ON_SCALAR = 44
W1_ON_SCALAR = 48
W2_ON_SCALAR = 0


def tile_picked_ylnkpr_rank_p_kernel(
    tc, x_words, x_scales, w1, w2, e_words, e_scales, w3, unit, unit2, dt, offs, tgt, ls, neg_, out
):
    nc = tc.nc
    with ExitStack() as ctx:
        keep = ctx.enter_context(tc.tile_pool(name="keep", bufs=1))
        psum = ctx.enter_context(tc.psum_pool(name="psum", bufs=1))

        def load_list(name, dram):
            held = keep.tile([P, dram.shape[1]], U16, name=name)
            nc.sync.dma_start(held[:], dram)
            return held

        def load_words(name, dram, width):
            table = keep.tile([P, width], I32, name=name, tag=name)
            nc.sync.dma_start(table[:], dram[0].rearrange("p n t -> p (n t)").bitcast(I32))
            return table

        def load_scales(queue, table, dram, first):
            for r in range(4):
                queue.dma_start(table[first + r : P : 32, :].bitcast(I32), dram[0, r:16:4, :].bitcast(I32))

        def load_weight(name, dram):
            raw = keep.tile([P, PACK, H], F32, name=name, tag=name)
            nc.sync.dma_start(raw[:], dram.rearrange("(p j) c -> p j c", j=PACK))
            return raw

        def load_factors(name, dram):
            held = keep.tile([P, PACK], F32, name=name)
            nc.sync.dma_start(held[:], dram.rearrange("(p t) o -> p (t o)", t=PACK))
            return held

        def gather(name, table, dtype, offsets, tag):
            picked = keep.tile([P, S], dtype, name=name, tag=tag, align_bytes=64)
            nc.vector.tensor_copy(picked[:], table.indirect(offsets[:]))
            return picked

        def cast_weight(name, raw, on_scalar):
            grouped = keep.tile([P, PACK, P, PACK], BF16, name=name, tag=name, align_bytes=64)
            dst = grouped[:].rearrange("p t m j -> p m j t")
            src = raw[:].rearrange("p j (m t) -> p m j t", t=PACK)
            if on_scalar > 0:
                nc.scalar.copy(dst[:, :on_scalar], src[:, :on_scalar])
            nc.vector.tensor_copy(dst[:, on_scalar:], src[:, on_scalar:])
            return grouped

        def quantize(name, values, width):
            codes = keep.tile([P, width], U32, name=name + "_codes", align_bytes=64)
            scales = keep.tile([P, width], U8, name=name + "_scales", align_bytes=64)
            nc.vector.quantize_mx(out=codes[:].bitcast(FP8X4), scales=scales[:], in_=values)
            return codes, scales

        def product(acc, lhs, lhs_cols, rhs, rhs_cols):
            nc.tensor.matmul_mx(
                out=acc,
                lhsT=lhs[0][:, lhs_cols].bitcast(FP8X4),
                lhsT_scale=lhs[1][:, lhs_cols],
                rhs=rhs[0][:, rhs_cols].bitcast(FP8X4),
                rhs_scale=rhs[1][:, rhs_cols],
                start=True,
                stop=True,
            )

        def block(n):
            return slice(n * P, (n + 1) * P)

        def list_half(held, h):
            return held[:, h * (HALF // 16) : (h + 1) * (HALF // 16)]

        def half(h):
            return slice(h * HALF, (h + 1) * HALF)

        xs_table = keep.tile([P, T], U8, name="xs_table")
        es_table = keep.tile([P, W], U8, name="es_table")
        nc.gpsimd.memset(xs_table[:].bitcast(I32), 0)
        nc.gpsimd.memset(es_table[:].bitcast(I32), 0)

        xw_table = load_words("xw_table", x_words, T)
        offs_sb = load_list("offs_sb", offs)
        load_scales(nc.sync, xs_table, x_scales, 4)
        w1_raw = load_weight("w1_raw", w1)
        tgt_sb = load_list("tgt_sb", tgt)
        load_scales(nc.sync, es_table, e_scales, 0)
        unit_sb = load_factors("unit_sb", unit)
        w2_raw = load_weight("w2_raw", w2)
        ls_sb = load_list("ls_sb", ls)
        w3_raw = load_weight("w3_raw", w3)
        ew_table = load_words("ew_table", e_words, W)
        unit2_sb = load_factors("unit2_sb", unit2)
        neg_sb = load_list("neg_sb", neg_)
        dt_sb = keep.tile([P, W], F32, name="dt_sb")
        nc.sync.dma_start(dt_sb[:], dt)
        half_unit = keep.tile([P, PACK], F32, name="half_unit")
        nc.gpsimd.tensor_scalar(half_unit[:], unit_sb[:], 0.5, 0.0, ALU.mult, ALU.add)

        xw = gather("xw", xw_table[:].bitcast(U32), U32, offs_sb, "xw")
        xs = gather("xs", xs_table[:], U8, offs_sb, "xs")
        w1_b = cast_weight("w1_b", w1_raw, W1_ON_SCALAR)
        xq = (xw, xs[4:P])
        w1q = quantize("w1", w1_b[:].rearrange("p t m j -> p (t m j)"), H)
        y_banks = []
        for t in range(PACK):
            bank = psum.tile([P, S], F32, name="y%d" % t, tag="b%d" % t)
            product(bank[:], w1q, block(t), xq, slice(0, S))
            y_banks.append(bank)
        w2_b = cast_weight("w2_b", w2_raw, W2_ON_SCALAR)
        y_half = keep.tile([P, PACK, S], F32, name="y_half")
        w2q = quantize("w2", w2_b[:].rearrange("p t m j -> p (t m j)"), H)
        yg_banks = []
        for t in range(PACK):
            bank = psum.tile([P, S], F32, name="yg%d" % t, tag="a%d" % t)
            product(bank[:], w2q, block(t), xq, slice(0, S))
            yg_banks.append(bank)
        w3_b = cast_weight("w3_b", w3_raw, W3_ON_SCALAR)
        w3q = quantize("w3", w3_b[:].rearrange("p t m j -> p (t m j)"), H)
        for t in range(PACK):
            nc.scalar.activation(y_half[:, t, :], y_banks[t][:], ACT.Copy, scale=half_unit[:, t : t + 1])
        es = gather("es", es_table[:], U8, tgt_sb, "w1_b")
        ew = gather("ew", ew_table[:].bitcast(U32), U32, tgt_sb, "ew")
        eq = (ew, es)

        tanh_yg = keep.tile([P, PACK, S], F32, name="tanh_yg", tag="w3_raw")
        gated0 = keep.tile([P, PACK, HALF], F32, name="gated0", tag="ew_table")
        for t in range(PACK):
            nc.scalar.activation(tanh_yg[:, t, :], yg_banks[t][:], ACT.Tanh, scale=0.5)
            nc.vector.scalar_tensor_tensor(
                gated0[:, t, :], tanh_yg[:, t, half(0)], 1.0, y_half[:, t, half(0)], ALU.add, ALU.mult
            )

        hid2_b = keep.tile([P, Z, PACK], BF16, name="hid2_b", tag="hid2_b", align_bytes=64)
        tst = []
        for c in range(4):
            bank = psum.tile([P, PACK, P], F32, name="ye%d" % c, tag="b%d" % c)
            for t in range(PACK):
                product(bank[:, t, :], w3q, block(t), eq, block(c))
            ye = bank[:].rearrange("p t n -> p n t")
            tanh_ye = keep.tile([P, P, PACK], F32, name="tanh_ye%d" % c, tag=("picked0", "picked1", "fade", "ye3")[c])
            nc.scalar.activation(tanh_ye[:], ye, ACT.Tanh)
            total = keep.tile([P, P, PACK], F32, name="tst%d" % c)
            nc.vector.scalar_tensor_tensor(total[:], ye, 0.3, tanh_ye[:], ALU.mult, ALU.add)
            tst.append(total)
        for c in range(4):
            nc.vector.tensor_tensor(
                hid2_b[:, block(c), :], tst[c][:], unit2_sb[:].unsqueeze(1).to_broadcast([P, P, PACK]), ALU.mult
            )

        def pick_half(h):
            picked = keep.tile([P, PACK, HALF], F32, name="picked%d" % h, tag="picked%d" % h)
            for t in range(PACK):
                nc.scalar.activation(picked[:, t, :], y_half[:, t, :].indirect(list_half(ls_sb, h)), ACT.Copy)
            return picked

        def hid_half(h, gated, picked):
            hid_b = keep.tile([P, HALF, PACK], BF16, name="hid_b%d" % h, align_bytes=64)
            nc.vector.tensor_tensor(
                hid_b[:].rearrange("p (c i) t -> p c t i", i=2),
                gated[:].rearrange("p t (c i) -> p c t i", i=2),
                picked[:].rearrange("p t (c i) -> p c t i", i=2),
                ALU.add,
            )
            return hid_b

        hid_b0 = hid_half(0, gated0, pick_half(0))
        hid2q = quantize("hid2", hid2_b[:].rearrange("p n t -> p (n t)"), Z)
        fade = keep.tile([P, Z], F32, name="fade", tag="fade")
        nc.scalar.activation(fade[:], dt_sb[:].indirect(tgt_sb[:]), ACT.Exp, scale=-1.0)

        staged = keep.tile([P, 4, Z], F32, name="staged")
        grown = keep.tile([P, 4, Z], F32, name="grown")

        def scores(r, hidq):
            bank = psum.tile([P, Z], F32, name="sc%d" % r, tag="a%d" % r)
            product(bank[:], hidq, block(r % 2), hid2q, slice(0, Z))
            dec = keep.tile([P, Z], F32, name="dec%d" % r)
            nc.vector.tensor_tensor(dec[:], bank[:], fade[:], ALU.mult)
            return dec

        def spread(r, first, count):
            return staged[:, :, r * P + first // 4 : r * P + (first + count) // 4]

        def bound(r, first, count):
            source = marg[r][:, first : first + count].rearrange("p (a n) -> p a n", a=4)
            nc.scalar.activation(spread(r, first, count), source, ACT.Tanh)

        def grow(r, first, count):
            target = grown[:, r, first : first + count].rearrange("p (a n) -> p a n", a=4)
            nc.scalar.activation(target, spread(r, first, count), ACT.Exp, scale=1.5)

        other = [keep.tile([P, Z], F32, name="other%d" % r) for r in range(4)]
        marg = [keep.tile([P, Z], F32, name="marg%d" % r) for r in range(4)]

        hidq0 = quantize("hid0", hid_b0[:].rearrange("p n t -> p (n t)"), HALF)
        picked1 = pick_half(1)
        gated1 = keep.tile([P, PACK, HALF], F32, name="gated1", tag="hid2_b", align_bytes=64)
        nc.vector.scalar_tensor_tensor(gated1[:], tanh_yg[:, :, half(1)], 1.0, y_half[:, :, half(1)], ALU.add, ALU.mult)
        decs = [scores(r, hidq0) for r in range(2)]
        hid_b1 = hid_half(1, gated1, picked1)
        hidq1 = quantize("hid1", hid_b1[:].rearrange("p n t -> p (n t)"), HALF)
        for r in range(2):
            for h in range(2):
                nc.scalar.activation(other[r][:, half(h)], decs[r][:].indirect(list_half(neg_sb, h)), ACT.Copy)
            nc.vector.tensor_tensor(marg[r][:], other[r][:], decs[r][:], ALU.subtract)
        for r in range(2):
            bound(r, 0, Z)
        for r in range(2):
            grow(r, 0, Z)
        decs = decs + [scores(r, hidq1) for r in range(2, 4)]
        for r in range(2, 4):
            nc.vector.tensor_copy(other[r][:], decs[r][:])
        for h in range(2):
            for r in range(2, 4):
                nc.vector.tensor_tensor(
                    marg[r][:, half(h)], decs[r][:].indirect(list_half(neg_sb, h)), other[r][:, half(h)], ALU.subtract
                )
                bound(r, h * HALF, HALF)
            for r in range(2, 4):
                grow(r, h * HALF, HALF)

        for r in range(3):
            nc.scalar.activation(staged[:, r, :], grown[:, r, :], ACT.Ln, bias=0.5)
            nc.sync.dma_start(out[block(r), :], staged[:, r, :])
        for h in range(2):
            nc.scalar.activation(staged[:, 3, half(h)], grown[:, 3, half(h)], ACT.Ln, bias=0.5)
            nc.sync.dma_start(out[block(3), half(h)], staged[:, 3, half(h)])
